import numpy as np
import ml_dtypes


def mxq(x, axis, fmt="e4m3"):
    dtype, down = {"e4m3": (ml_dtypes.float8_e4m3fn, 7), "e5m2": (ml_dtypes.float8_e5m2, 14)}[fmt]
    v = np.moveaxis(np.asarray(x, np.float32).astype(ml_dtypes.bfloat16).astype(np.float64), axis, -1)
    blocks = v.reshape(v.shape[:-1] + (-1, 32))
    amax = np.abs(blocks).max(-1, keepdims=True)
    byte = np.maximum(np.where(amax > 0, np.frexp(amax)[1] - 1 + 127, 0) - down, 1)
    scale = np.exp2(byte - 127.0)
    codes = (blocks / scale).astype(np.float32).astype(dtype).astype(np.float64)
    return np.moveaxis((codes * scale).reshape(v.shape), -1, axis)


WIDE = False


def mx_kscale(k):
    if not WIDE:
        return np.ones(k)
    levels = np.array([10, -10, 5, -5, 0])
    if k % 512:
        return np.exp2(np.random.permutation(np.resize(levels, k // 32))).repeat(32)
    a = np.empty((k // 512, 16))
    for p in range(k // 512):
        a[p, :8] = np.random.permutation(np.resize(levels, 8))
        for g in range(8):
            far = levels[np.abs(levels - a[p, g]) >= 10]
            a[p, g + 8] = far[np.random.randint(len(far))]
    return np.exp2(a.ravel()).repeat(32)


def f64(x):
    return np.asarray(x).astype(np.float64)


def striped(idx):
    return np.tile(np.asarray(idx).reshape(-1, 16).T, (8, 1)).astype(np.uint16)


def unstriped(offs):
    return offs[:16].T.reshape(-1).astype(np.int64)


E2M1 = np.array([0.0, 0.5, 1.0, 1.5, 2.0, 3.0, 4.0, 6.0, -0.0, -0.5, -1.0, -1.5, -2.0, -3.0, -4.0, -6.0])


def pack_weight(w, fmt):
    k, n = w.shape
    w = f64(np.asarray(w, np.float32).astype(ml_dtypes.bfloat16)).reshape(k // 32, 32, n)
    amax = np.abs(w).max(1)
    if fmt == "e4m3":
        byte = np.frexp(amax)[1] - 1 + 127 - 7
    else:
        mant, ex = np.frexp(amax / 6.0)
        byte = np.where(mant > 0.5, ex, ex - 1) + 127
    byte = np.clip(np.where(amax > 0, byte, 1), 1, 254)
    scaled = (w * np.exp2(127.0 - byte)[:, None, :]).reshape(k, n).astype(np.float32)
    by_word = np.ascontiguousarray(scaled.reshape(k // 512, 128, 4, n).transpose(0, 1, 3, 2))
    if fmt == "e4m3":
        words = by_word.astype(ml_dtypes.float8_e4m3fn).view(np.uint8)
    else:
        c = by_word.astype(ml_dtypes.float4_e2m1fn).view(np.uint8) & 0xF
        words = (c[..., 0::2] | (c[..., 1::2] << 4)).reshape(k // 512, 128, 2 * n)
    return np.ascontiguousarray(words), np.ascontiguousarray(byte.astype(np.uint8).reshape(k // 512, 16, n))


def unpack_weight(words, scales, fmt):
    g, _, n = scales.shape
    words = np.ascontiguousarray(words).reshape(g, 128, n, -1)
    if fmt == "e4m3":
        vals = words.view(ml_dtypes.float8_e4m3fn).astype(np.float64)
    else:
        nib = np.empty((g, 128, n, 4), np.uint8)
        nib[..., 0::2] = words & 0xF
        nib[..., 1::2] = words >> 4
        vals = E2M1[nib]
    vals = vals * np.repeat(np.exp2(scales.astype(np.float64) - 127.0), 8, axis=1)[..., None]
    return vals.transpose(0, 1, 3, 2).reshape(g * 512, n)


def bf(x):
    return np.asarray(x, np.float32).astype(ml_dtypes.bfloat16)


def planes(Y):
    r, m = Y.shape
    b = f64(bf(Y)).reshape(r // 32, 32, m)
    amax = np.abs(b).max(1)
    byte = np.clip(np.where(amax > 0, np.frexp(amax)[1] - 1 + 127 - 7, 1), 1, 254)
    codes = (b * np.exp2(127.0 - byte)[:, None, :]).reshape(r, m).astype(np.float32).astype(ml_dtypes.float8_e4m3fn).view(np.uint8)
    words = codes.reshape(r // 512, 128, 4, m).transpose(0, 1, 3, 2)
    return np.ascontiguousarray(words), np.ascontiguousarray(byte.astype(np.uint8).reshape(r // 512, 16, m))


K, V, T, J, N = 512, 512, 1024, 512, 512


def setup_inputs():
    n = np.random.standard_normal
    idx = np.random.permutation(T)[:J]
    idx2 = np.random.randint(0, V, J)
    fk = mx_kscale(K)
    pqp = pack_weight(n((K, V)) / fk[:, None], "e2m1")
    wqp = pack_weight(n((K, N)) * 1 / np.sqrt(K) * fk[:, None], "e4m3")
    wfp = pack_weight(n((K, N)) * 1 / np.sqrt(K) * fk[:, None], "e2m1")
    return {
        "pq_words": pqp[0],
        "pq_scales": pqp[1],
        "wq_words": wqp[0],
        "wq_scales": wqp[1],
        "xf": (n((K, T)) / fk[:, None]).astype(np.float32),
        "pf": (n((K, V)) / fk[:, None]).astype(np.float32),
        "wf_words": wfp[0],
        "wf_scales": wfp[1],
        "offs": striped(idx),
        "offs2": striped(idx2),
    }


def reference(pq_words, pq_scales, wq_words, wq_scales, xf, pf, wf_words, wf_scales, offs, offs2):
    idx = unstriped(offs)
    idx2 = unstriped(offs2)
    pqu = unpack_weight(pq_words, pq_scales, "e2m1")
    wqu = unpack_weight(wq_words, wq_scales, "e4m3")
    wfu = unpack_weight(wf_words, wf_scales, "e2m1")
    z = wqu.T @ pqu
    d = f64(xf)[:, idx] - f64(pf)[:, idx2]
    dq = mxq(d, 0, "e4m3")
    p = wfu.T @ dq
    y = z[:, idx2] + np.tanh(p)
    words, scales = planes(y)
    return y, words, scales

@@ -1,0 +1,223 @@
+from contextlib import ExitStack
+
+import concourse.mybir as mybir
+
+K, V, T, J, N = 512, 512, 1024, 512, 512
+FLOPS = 2 * K * N * (V + J)
+
+F32 = mybir.dt.float32
+BF16 = mybir.dt.bfloat16
+I32 = mybir.dt.int32
+U32 = mybir.dt.uint32
+U16 = mybir.dt.uint16
+U8 = mybir.dt.uint8
+FP8X4 = mybir.dt.float8_e4m3fn_x4
+FP4X4 = mybir.dt.float4_e2m1fn_x4
+ALU = mybir.AluOpType
+TANH = mybir.ActivationFunctionType.Tanh
+
+P = 128
+PACK = 4
+HALF = J // 2
+STRIPE = 16
+
+
+def tile_list_remainder_on_prototype_pl_kernel(
+    tc, pq_words, pq_scales, wq_words, wq_scales, xf, pf, wf_words, wf_scales, offs, offs2, out_0, out_1, out_2
+):
+    nc = tc.nc
+    with ExitStack() as ctx:
+        sb = ctx.enter_context(tc.tile_pool(name="sb", bufs=1))
+        ps = ctx.enter_context(tc.psum_pool(name="ps", bufs=2))
+
+        def tile(name, shape, dtype):
+            return sb.tile(shape, dtype, name=name, align_bytes=64)
+
+        tok_list = tile("tok_list", [P, J // STRIPE], U16)
+        proto_list = tile("proto_list", [P, J // STRIPE], U16)
+        pf_first = tile("pf_first", [P, V], F32)
+        pf_rest = tile("pf_rest", [P, (PACK - 1) * V], F32)
+        xf_sb = [tile(f"xf{t}", [P, T], F32) for t in range(PACK)]
+        wq_raw = tile("wq_raw", [P, N], I32)
+        wf_raw = tile("wf_raw", [P, 2 * N], U8)
+        pq_sb = tile("pq_sb", [P, 2 * V], U8)
+        scale_raw = tile("scale_raw", [P, 3 * N], U8)
+        wq_sc_raw, wf_sc_raw, pq_sc = (scale_raw[:, i * N : (i + 1) * N] for i in range(3))
+        wq_dealt = tile("wq_dealt", [P, N], U32)
+        wf_dealt = tile("wf_dealt", [P, 2 * N], U8)
+        wq_sc = tile("wq_sc", [P, N], U8)
+        wf_sc = tile("wf_sc", [P, N], U8)
+        warm = tile("warm", [P, 2], F32)
+
+        def half_list(lst, h):
+            cols = HALF // STRIPE
+            return lst[:, h * cols : (h + 1) * cols]
+
+        def load_scales(queue, dst, src):
+            for q in range(4):
+                queue.dma_start(out=dst[32 * q : 32 * q + 4, :].bitcast(I32), in_=src[0, 4 * q : 4 * q + 4, :].bitcast(I32))
+
+        nc.gpsimd.memset(scale_raw[:].bitcast(I32), 0)
+        nc.vector.memset(warm[:, 0:1], 0.0)
+        nc.scalar.activation(out=warm[:, 1:2], in_=warm[:, 0:1], func=TANH)
+
+        pf_rows = pf.rearrange("(p t) v -> p (t v)", t=PACK)
+        xf_rows = xf.rearrange("(p t) c -> p t c", t=PACK)
+        nc.sync.dma_start(proto_list[:], offs2)
+        nc.sync.dma_start(out=pf_first[:], in_=pf_rows[:, 0:V])
+        nc.sync.dma_start(tok_list[:], offs)
+        nc.sync.dma_start(out=xf_sb[0][:], in_=xf_rows[:, 0, :])
+        nc.sync.dma_start(out=wq_raw[:], in_=wq_words[0].rearrange("p n r -> p (n r)").bitcast(I32))
+        nc.sync.dma_start(out=pf_rest[:], in_=pf_rows[:, V:])
+        nc.sync.dma_start(out=xf_sb[1][:], in_=xf_rows[:, 1, :])
+        nc.sync.dma_start(out=pq_sb[:].bitcast(I32), in_=pq_words[0].bitcast(I32))
+        nc.sync.dma_start(out=xf_sb[2][:], in_=xf_rows[:, 2, :])
+        nc.sync.dma_start(out=wf_raw[:].bitcast(I32), in_=wf_words[0].bitcast(I32))
+        nc.sync.dma_start(out=xf_sb[3][:], in_=xf_rows[:, 3, :])
+        load_scales(nc.scalar, wq_sc_raw, wq_scales)
+        load_scales(nc.scalar, pq_sc, pq_scales)
+        load_scales(nc.scalar, wf_sc_raw, wf_scales)
+
+        def pf_window(t):
+            return pf_first[:] if t == 0 else pf_rest[:, (t - 1) * V : t * V]
+
+        picked_early = tile("picked_early", [P, 5 * HALF], F32)
+        picked_late = tile("picked_late", [P, 2 * HALF], F32)
+        picked = {}
+        for i, key in enumerate([(0, 0), (0, 1), (1, 0), (1, 1), (2, 0)]):
+            picked[key] = picked_early[:, i * HALF : (i + 1) * HALF]
+        picked[(3, 0)] = picked_late[:, HALF // 2 : HALF // 2 + HALF]
+        picked[(2, 1)] = picked_late[:, 0:HALF]
+        picked[(3, 1)] = picked_late[:, HALF:]
+
+        diff = [tile(f"diff{h}", [P, PACK * HALF], F32) for h in range(2)]
+        th0_ext = tile("th0_ext", [P, (PACK + 1) * HALF], F32)
+        th = [th0_ext[:, HALF:], tile("th1", [P, PACK * HALF], F32)[:]]
+        diff_bf = [diff[1][:, 2 * HALF :].bitcast(BF16), th0_ext[:, 0 : 2 * HALF].bitcast(BF16)]
+        d_codes = [tile(f"d_codes{h}", [P, HALF], U32) for h in range(2)]
+        d_sc = [tile(f"d_sc{h}", [P, HALF], U8) for h in range(2)]
+        z_sb = [tile(f"z{t}", [P, V], F32) for t in range(PACK)]
+        y = [tile(f"y{h}", [P, PACK * HALF], F32) for h in range(2)]
+        y_bf = [tile(f"y_bf{h}", [P, PACK * HALF], BF16) for h in range(2)]
+        y_codes = [tile(f"y_codes{h}", [P, HALF], U32) for h in range(2)]
+        y_sc = tile("y_sc", [P, J], U8)
+
+        def cols(t):
+            return slice(t * HALF, (t + 1) * HALF)
+
+        def pick_proto(t, h):
+            nc.vector.tensor_copy(picked[(t, h)], pf_window(t).indirect(half_list(proto_list, h)))
+
+        def remainder(t, h):
+            nc.vector.tensor_tensor(
+                diff[h][:, cols(t)], xf_sb[t][:].indirect(half_list(tok_list, h)), picked[(t, h)], ALU.subtract
+            )
+
+        def weave(copy, dst, src):
+            copy(
+                out=dst.rearrange("p (c i t) -> p c t i", i=4, t=PACK),
+                in_=src.rearrange("p (t c i) -> p c t i", i=4, t=PACK),
+            )
+
+        def deal(dst, src, width):
+            nc.vector.tensor_copy(
+                out=dst.rearrange("p (t m b) -> p m t b", t=PACK, b=width),
+                in_=src.rearrange("p (m t b) -> p m t b", t=PACK, b=width),
+            )
+
+        def product(t, h):
+            acc = ps.tile([P, HALF], F32, name=f"p{t}{h}", tag=f"bank{t}")
+            nc.tensor.matmul_mx(
+                out=acc[:],
+                lhsT=wf_dealt[:, 2 * P * t : 2 * P * (t + 1)].bitcast(FP4X4),
+                lhsT_scale=wf_sc[:, P * t : P * (t + 1)],
+                rhs=d_codes[h][:].bitcast(FP8X4),
+                rhs_scale=d_sc[h][:],
+                start=True,
+                stop=True,
+            )
+            return acc
+
+        def squash(t, h, acc):
+            nc.scalar.activation(out=th[h][:, cols(t)], in_=acc[:], func=TANH)
+
+        def add_features(t, h):
+            nc.vector.tensor_tensor(
+                y[h][:, cols(t)], z_sb[t][:].indirect(half_list(proto_list, h)), th[h][:, cols(t)], ALU.add
+            )
+
+        out_rows = out_0.rearrange("(p t) j -> p t j", t=PACK)
+        out_words = out_1[0].rearrange("p c r -> p (c r)").bitcast(I32)
+
+        def store_y(h, t0, t1):
+            nc.sync.dma_start(
+                out=out_rows[:, t0:t1, cols(h)],
+                in_=y[h][:, t0 * HALF : t1 * HALF].rearrange("p (t j) -> p t j", j=HALF),
+            )
+
+        def quantise_y(h):
+            nc.vector.quantize_mx(out=y_codes[h][:].bitcast(FP8X4), scales=y_sc[:, cols(h)], in_=y_bf[h][:])
+            nc.sync.dma_start(out=out_words[:, cols(h)], in_=y_codes[h][:].bitcast(I32))
+
+        for h in range(2):
+            pick_proto(0, h)
+        for h in range(2):
+            remainder(0, h)
+
+        deal(wq_dealt[:].bitcast(I32), wq_raw[:], 1)
+        deal(wq_sc[:], wq_sc_raw, 1)
+        for t in range(PACK):
+            acc = ps.tile([P, V], F32, name=f"zacc{t}", tag=f"bank{t}")
+            nc.tensor.matmul_mx(
+                out=acc[:],
+                lhsT=wq_dealt[:, P * t : P * (t + 1)].bitcast(FP8X4),
+                lhsT_scale=wq_sc[:, P * t : P * (t + 1)],
+                rhs=pq_sb[:].bitcast(FP4X4),
+                rhs_scale=pq_sc,
+                start=True,
+                stop=True,
+            )
+            nc.scalar.copy(out=z_sb[t][:], in_=acc[:])
+
+        for t, h in ((1, 0), (2, 0), (3, 0), (1, 1)):
+            pick_proto(t, h)
+        for t, h in ((1, 0), (1, 1), (2, 0), (3, 0)):
+            remainder(t, h)
+        weave(nc.scalar.copy, diff_bf[0], diff[0][:])
+        pick_proto(2, 1)
+        pick_proto(3, 1)
+        deal(wf_dealt[:], wf_raw[:], 2)
+        deal(wf_sc[:], wf_sc_raw, 1)
+        nc.vector.quantize_mx(out=d_codes[0][:].bitcast(FP8X4), scales=d_sc[0][:], in_=diff_bf[0])
+        remainder(2, 1)
+        remainder(3, 1)
+
+        accs = [product(t, 0) for t in range(PACK)]
+        squash(0, 0, accs[0])
+        add_features(0, 0)
+        squash(1, 0, accs[1])
+        squash(2, 0, accs[2])
+        weave(nc.scalar.copy, diff_bf[1], diff[1][:])
+        squash(3, 0, accs[3])
+        add_features(1, 0)
+        add_features(2, 0)
+        nc.vector.quantize_mx(out=d_codes[1][:].bitcast(FP8X4), scales=d_sc[1][:], in_=diff_bf[1])
+        add_features(3, 0)
+        store_y(0, 0, PACK)
+
+        accs = [product(t, 1) for t in range(PACK)]
+        for t in range(PACK):
+            squash(t, 1, accs[t])
+        weave(nc.scalar.copy, y_bf[0][:], y[0][:])
+        for t in range(PACK):
+            add_features(t, 1)
+            if t % 2 == 1:
+                store_y(1, t - 1, t + 1)
+        quantise_y(0)
+        weave(nc.vector.tensor_copy, y_bf[1][:], y[1][:])
+        quantise_y(1)
+        for q in range(4):
+            queue = nc.sync if q % 2 else nc.scalar
+            queue.dma_start(
+                out=out_2[0, 4 * q : 4 * q + 4, :].bitcast(I32), in_=y_sc[32 * q : 32 * q + 4, :].bitcast(I32)
+            )

@@ -1,6 +1,7 @@
 from contextlib import ExitStack
 
 import concourse.mybir as mybir
+from concourse.masks import make_identity
 
 K, V, T, J, N = 512, 512, 1024, 512, 512
 FLOPS = 2 * K * N * (V + J)
@@ -28,24 +29,25 @@ def tile_list_remainder_on_prototype_pl_kernel(
     nc = tc.nc
     with ExitStack() as ctx:
         sb = ctx.enter_context(tc.tile_pool(name="sb", bufs=1))
+        reuse = ctx.enter_context(tc.tile_pool(name="reuse", bufs=1))
         ps = ctx.enter_context(tc.psum_pool(name="ps", bufs=2))
 
-        def tile(name, shape, dtype):
-            return sb.tile(shape, dtype, name=name, align_bytes=64)
+        def tile(name, shape, dtype, tag=None):
+            return sb.tile(shape, dtype, name=name, tag=tag or name, align_bytes=64)
 
         tok_list = tile("tok_list", [P, J // STRIPE], U16)
         proto_list = tile("proto_list", [P, J // STRIPE], U16)
-        pf_first = tile("pf_first", [P, V], F32)
-        pf_rest = tile("pf_rest", [P, (PACK - 1) * V], F32)
+        pf_early = [tile(f"pf{t}", [P, V], F32) for t in range(2)]
+        pf_rest = tile("pf_rest", [P, 2 * V], F32)
         xf_sb = [tile(f"xf{t}", [P, T], F32) for t in range(PACK)]
-        wq_raw = tile("wq_raw", [P, N], I32)
+        wq_sb = tile("wq_sb", [P, N], U32)
         wf_raw = tile("wf_raw", [P, 2 * N], U8)
         pq_sb = tile("pq_sb", [P, 2 * V], U8)
-        scale_raw = tile("scale_raw", [P, 3 * N], U8)
-        wq_sc_raw, wf_sc_raw, pq_sc = (scale_raw[:, i * N : (i + 1) * N] for i in range(3))
-        wq_dealt = tile("wq_dealt", [P, N], U32)
+        wf_sc_raw = tile("wf_sc_raw", [P, N], U8)[:]
+        z_sc = tile("z_sc", [P, N + V], U8)
+        wq_sc, pq_sc = z_sc[:, 0:N], z_sc[:, N:]
+        ident = tile("ident", [P, P], F32)
         wf_dealt = tile("wf_dealt", [P, 2 * N], U8)
-        wq_sc = tile("wq_sc", [P, N], U8)
         wf_sc = tile("wf_sc", [P, N], U8)
         warm = tile("warm", [P, 2], F32)
 
@@ -57,48 +59,50 @@ def tile_list_remainder_on_prototype_pl_kernel(
             for q in range(4):
                 queue.dma_start(out=dst[32 * q : 32 * q + 4, :].bitcast(I32), in_=src[0, 4 * q : 4 * q + 4, :].bitcast(I32))
 
-        nc.gpsimd.memset(scale_raw[:].bitcast(I32), 0)
+        nc.gpsimd.memset(wf_sc_raw.bitcast(I32), 0)
         nc.vector.memset(warm[:, 0:1], 0.0)
-        nc.scalar.activation(out=warm[:, 1:2], in_=warm[:, 0:1], func=TANH)
 
         pf_rows = pf.rearrange("(p t) v -> p (t v)", t=PACK)
         xf_rows = xf.rearrange("(p t) c -> p t c", t=PACK)
+        nc.sync.dma_start(out=pf_early[0][:], in_=pf_rows[:, 0:V])
         nc.sync.dma_start(proto_list[:], offs2)
-        nc.sync.dma_start(out=pf_first[:], in_=pf_rows[:, 0:V])
+        nc.sync.dma_start(out=pf_early[1][:], in_=pf_rows[:, V : 2 * V])
         nc.sync.dma_start(tok_list[:], offs)
         nc.sync.dma_start(out=xf_sb[0][:], in_=xf_rows[:, 0, :])
-        nc.sync.dma_start(out=wq_raw[:], in_=wq_words[0].rearrange("p n r -> p (n r)").bitcast(I32))
-        nc.sync.dma_start(out=pf_rest[:], in_=pf_rows[:, V:])
-        nc.sync.dma_start(out=xf_sb[1][:], in_=xf_rows[:, 1, :])
+        nc.sync.dma_start(out=wq_sb[:].bitcast(I32), in_=wq_words[0].rearrange("p n r -> p (n r)").bitcast(I32))
         nc.sync.dma_start(out=pq_sb[:].bitcast(I32), in_=pq_words[0].bitcast(I32))
-        nc.sync.dma_start(out=xf_sb[2][:], in_=xf_rows[:, 2, :])
+        nc.sync.dma_start(out=pf_rest[:], in_=pf_rows[:, 2 * V :])
+        for t in range(1, PACK):
+            nc.sync.dma_start(out=xf_sb[t][:], in_=xf_rows[:, t, :])
         nc.sync.dma_start(out=wf_raw[:].bitcast(I32), in_=wf_words[0].bitcast(I32))
-        nc.sync.dma_start(out=xf_sb[3][:], in_=xf_rows[:, 3, :])
-        load_scales(nc.scalar, wq_sc_raw, wq_scales)
-        load_scales(nc.scalar, pq_sc, pq_scales)
-        load_scales(nc.scalar, wf_sc_raw, wf_scales)
+        nc.scalar.dma_start(out=wq_sc[0:16, :].bitcast(I32), in_=wq_scales[0].bitcast(I32))
+        nc.scalar.dma_start(out=pq_sc[0:16, :].bitcast(I32), in_=pq_scales[0].bitcast(I32))
+        for q in range(1, 4):
+            nc.scalar.dma_start(
+                out=z_sc[32 * q : 32 * q + 4, :].bitcast(I32), in_=z_sc[4 * q : 4 * q + 4, :].bitcast(I32)
+            )
+        nc.scalar.activation(out=warm[:, 1:2], in_=warm[:, 0:1], func=TANH)
+        make_identity(nc, ident[:])
+        load_scales(nc.gpsimd, wf_sc_raw, wf_scales)
 
         def pf_window(t):
-            return pf_first[:] if t == 0 else pf_rest[:, (t - 1) * V : t * V]
+            return pf_early[t][:] if t < 2 else pf_rest[:, (t - 2) * V : (t - 1) * V]
 
-        picked_early = tile("picked_early", [P, 5 * HALF], F32)
-        picked_late = tile("picked_late", [P, 2 * HALF], F32)
-        picked = {}
-        for i, key in enumerate([(0, 0), (0, 1), (1, 0), (1, 1), (2, 0)]):
-            picked[key] = picked_early[:, i * HALF : (i + 1) * HALF]
-        picked[(3, 0)] = picked_late[:, HALF // 2 : HALF // 2 + HALF]
-        picked[(2, 1)] = picked_late[:, 0:HALF]
-        picked[(3, 1)] = picked_late[:, HALF:]
+        picked_all = tile("picked", [P, 7 * HALF], F32)
+        picked = {(t, h): picked_all[:, (2 * t + h) * HALF : (2 * t + h + 1) * HALF] for t in range(3) for h in range(2)}
+        picked[(3, 0)] = picked[(3, 1)] = picked_all[:, 6 * HALF :]
 
-        diff = [tile(f"diff{h}", [P, PACK * HALF], F32) for h in range(2)]
-        th0_ext = tile("th0_ext", [P, (PACK + 1) * HALF], F32)
-        th = [th0_ext[:, HALF:], tile("th1", [P, PACK * HALF], F32)[:]]
-        diff_bf = [diff[1][:, 2 * HALF :].bitcast(BF16), th0_ext[:, 0 : 2 * HALF].bitcast(BF16)]
+        diff = [
+            reuse.tile([P, PACK * HALF], F32, name="diff0", offset=0),
+            tile("diff1", [P, PACK * HALF], F32),
+        ]
+        th = [tile(f"th{h}", [P, PACK * HALF], F32) for h in range(2)]
+        diff_bf = [diff[1][:, 2 * HALF :].bitcast(BF16)]
         d_codes = [tile(f"d_codes{h}", [P, HALF], U32) for h in range(2)]
         d_sc = [tile(f"d_sc{h}", [P, HALF], U8) for h in range(2)]
-        z_sb = [tile(f"z{t}", [P, V], F32) for t in range(PACK)]
+        z_sb = [tile(f"z{t}", [P, V], F32) for t in range(2)]
+        z_sb += [reuse.tile([P, V], F32, name=f"z{2 + i}", offset=4 * V * i) for i in range(2)]
         y = [tile(f"y{h}", [P, PACK * HALF], F32) for h in range(2)]
-        y_bf = [tile(f"y_bf{h}", [P, PACK * HALF], BF16) for h in range(2)]
         y_codes = [tile(f"y_codes{h}", [P, HALF], U32) for h in range(2)]
         y_sc = tile("y_sc", [P, J], U8)
 
@@ -159,34 +163,41 @@ def tile_list_remainder_on_prototype_pl_kernel(
             nc.vector.quantize_mx(out=y_codes[h][:].bitcast(FP8X4), scales=y_sc[:, cols(h)], in_=y_bf[h][:])
             nc.sync.dma_start(out=out_words[:, cols(h)], in_=y_codes[h][:].bitcast(I32))
 
-        for h in range(2):
-            pick_proto(0, h)
+        for t in range(2):
+            for h in range(2):
+                pick_proto(t, h)
         for h in range(2):
             remainder(0, h)
 
-        deal(wq_dealt[:].bitcast(I32), wq_raw[:], 1)
-        deal(wq_sc[:], wq_sc_raw, 1)
-        for t in range(PACK):
-            acc = ps.tile([P, V], F32, name=f"zacc{t}", tag=f"bank{t}")
+        zt_sb = [tile(f"zt{b}", [P, N], F32) for b in range(V // P)]
+        for b in range(V // P):
+            acc = ps.tile([P, N], F32, name=f"zt_acc{b}", tag=f"bank{b}")
             nc.tensor.matmul_mx(
                 out=acc[:],
-                lhsT=wq_dealt[:, P * t : P * (t + 1)].bitcast(FP8X4),
-                lhsT_scale=wq_sc[:, P * t : P * (t + 1)],
-                rhs=pq_sb[:].bitcast(FP4X4),
-                rhs_scale=pq_sc,
+                lhsT=pq_sb[:, 2 * P * b : 2 * P * (b + 1)].bitcast(FP4X4),
+                lhsT_scale=pq_sc[:, P * b : P * (b + 1)],
+                rhs=wq_sb[:].bitcast(FP8X4),
+                rhs_scale=wq_sc,
                 start=True,
                 stop=True,
             )
-            nc.scalar.copy(out=z_sb[t][:], in_=acc[:])
+            nc.scalar.copy(
+                out=zt_sb[b][:].rearrange("p (t m) -> p t m", t=PACK), in_=acc[:].rearrange("p (m t) -> p t m", t=PACK)
+            )
+        z_accs = [ps.tile([P, V], F32, name=f"z_acc{t}", tag=f"bank{t}") for t in range(PACK)]
+        for t in range(PACK):
+            for b in range(V // P):
+                nc.tensor.transpose(z_accs[t][:, P * b : P * (b + 1)], zt_sb[b][:, P * t : P * (t + 1)], ident[:])
 
-        for t, h in ((1, 0), (2, 0), (3, 0), (1, 1)):
+        for t, h in ((2, 0), (3, 0), (2, 1)):
             pick_proto(t, h)
         for t, h in ((1, 0), (1, 1), (2, 0), (3, 0)):
             remainder(t, h)
         weave(nc.scalar.copy, diff_bf[0], diff[0][:])
-        pick_proto(2, 1)
+        for t in range(PACK):
+            nc.scalar.copy(out=z_sb[t][:], in_=z_accs[t][:])
         pick_proto(3, 1)
-        deal(wf_dealt[:], wf_raw[:], 2)
+        deal(wf_dealt[:].bitcast(U16), wf_raw[:].bitcast(U16), 1)
         deal(wf_sc[:], wf_sc_raw, 1)
         nc.vector.quantize_mx(out=d_codes[0][:].bitcast(FP8X4), scales=d_sc[0][:], in_=diff_bf[0])
         remainder(2, 1)
@@ -196,18 +207,20 @@ def tile_list_remainder_on_prototype_pl_kernel(
         squash(0, 0, accs[0])
         add_features(0, 0)
         squash(1, 0, accs[1])
-        squash(2, 0, accs[2])
+        diff_bf.append(tile("diff_bf1", [P, PACK * HALF], BF16, tag="d_codes0")[:])
         weave(nc.scalar.copy, diff_bf[1], diff[1][:])
+        squash(2, 0, accs[2])
         squash(3, 0, accs[3])
         add_features(1, 0)
-        add_features(2, 0)
         nc.vector.quantize_mx(out=d_codes[1][:].bitcast(FP8X4), scales=d_sc[1][:], in_=diff_bf[1])
+        add_features(2, 0)
         add_features(3, 0)
         store_y(0, 0, PACK)
 
         accs = [product(t, 1) for t in range(PACK)]
         for t in range(PACK):
             squash(t, 1, accs[t])
+        y_bf = [tile("y_bf0", [P, PACK * HALF], BF16, tag="d_codes1"), tile("y_bf1", [P, PACK * HALF], BF16)]
         weave(nc.scalar.copy, y_bf[0][:], y[0][:])
         for t in range(PACK):
             add_features(t, 1)

@@ -21,6 +21,7 @@ P = 128
 PACK = 4
 HALF = J // 2
 STRIPE = 16
+WIDE = 704
 
 
 def tile_list_remainder_on_prototype_pl_kernel(
@@ -37,15 +38,15 @@ def tile_list_remainder_on_prototype_pl_kernel(
 
         tok_list = tile("tok_list", [P, J // STRIPE], U16)
         proto_list = tile("proto_list", [P, J // STRIPE], U16)
-        pf_early = [tile(f"pf{t}", [P, V], F32) for t in range(2)]
+        pf_early = tile("pf_early", [P, V + WIDE], F32)
         pf_rest = tile("pf_rest", [P, 2 * V], F32)
         xf_sb = [tile(f"xf{t}", [P, T], F32) for t in range(PACK)]
         wq_sb = tile("wq_sb", [P, N], U32)
         wf_raw = tile("wf_raw", [P, 2 * N], U8)
         pq_sb = tile("pq_sb", [P, 2 * V], U8)
         wf_sc_raw = tile("wf_sc_raw", [P, N], U8)[:]
-        z_sc = tile("z_sc", [P, N + V], U8)
-        wq_sc, pq_sc = z_sc[:, 0:N], z_sc[:, N:]
+        wq_sc = tile("wq_sc", [P, N], U8)[:]
+        pq_sc = tile("pq_sc", [P, V], U8)[:]
         ident = tile("ident", [P, P], F32)
         wf_dealt = tile("wf_dealt", [P, 2 * N], U8)
         wf_sc = tile("wf_sc", [P, N], U8)
@@ -55,38 +56,36 @@ def tile_list_remainder_on_prototype_pl_kernel(
             cols = HALF // STRIPE
             return lst[:, h * cols : (h + 1) * cols]
 
-        def load_scales(queue, dst, src):
-            for q in range(4):
-                queue.dma_start(out=dst[32 * q : 32 * q + 4, :].bitcast(I32), in_=src[0, 4 * q : 4 * q + 4, :].bitcast(I32))
+        def load_scales(dst, src, quadrants=range(4)):
+            for q in quadrants:
+                nc.sync.dma_start(out=dst[32 * q : 32 * q + 4, :].bitcast(I32), in_=src[0, 4 * q : 4 * q + 4, :].bitcast(I32))
 
-        nc.gpsimd.memset(wf_sc_raw.bitcast(I32), 0)
+        nc.vector.memset(wf_sc_raw.bitcast(I32), 0)
         nc.vector.memset(warm[:, 0:1], 0.0)
+        nc.vector.memset(pf_early[:, 2 * V :], 0.0)
 
         pf_rows = pf.rearrange("(p t) v -> p (t v)", t=PACK)
         xf_rows = xf.rearrange("(p t) c -> p t c", t=PACK)
-        nc.sync.dma_start(out=pf_early[0][:], in_=pf_rows[:, 0:V])
+        nc.sync.dma_start(out=pf_early[:, V : 2 * V], in_=pf_rows[:, 0:V])
         nc.sync.dma_start(proto_list[:], offs2)
-        nc.sync.dma_start(out=pf_early[1][:], in_=pf_rows[:, V : 2 * V])
+        load_scales(wq_sc, wq_scales, range(3))
+        nc.sync.dma_start(out=pf_early[:, 0:V], in_=pf_rows[:, V : 2 * V])
         nc.sync.dma_start(tok_list[:], offs)
         nc.sync.dma_start(out=xf_sb[0][:], in_=xf_rows[:, 0, :])
+        load_scales(wq_sc, wq_scales, range(3, 4))
+        nc.sync.dma_start(out=pf_rest[:], in_=pf_rows[:, 2 * V :])
+        load_scales(pq_sc, pq_scales)
         nc.sync.dma_start(out=wq_sb[:].bitcast(I32), in_=wq_words[0].rearrange("p n r -> p (n r)").bitcast(I32))
         nc.sync.dma_start(out=pq_sb[:].bitcast(I32), in_=pq_words[0].bitcast(I32))
-        nc.sync.dma_start(out=pf_rest[:], in_=pf_rows[:, 2 * V :])
-        for t in range(1, PACK):
+        for t in range(1, 3):
             nc.sync.dma_start(out=xf_sb[t][:], in_=xf_rows[:, t, :])
+        load_scales(wf_sc_raw, wf_scales)
+        nc.sync.dma_start(out=xf_sb[3][:], in_=xf_rows[:, 3, :])
         nc.sync.dma_start(out=wf_raw[:].bitcast(I32), in_=wf_words[0].bitcast(I32))
-        nc.scalar.dma_start(out=wq_sc[0:16, :].bitcast(I32), in_=wq_scales[0].bitcast(I32))
-        nc.scalar.dma_start(out=pq_sc[0:16, :].bitcast(I32), in_=pq_scales[0].bitcast(I32))
-        for q in range(1, 4):
-            nc.scalar.dma_start(
-                out=z_sc[32 * q : 32 * q + 4, :].bitcast(I32), in_=z_sc[4 * q : 4 * q + 4, :].bitcast(I32)
-            )
         nc.scalar.activation(out=warm[:, 1:2], in_=warm[:, 0:1], func=TANH)
         make_identity(nc, ident[:])
-        load_scales(nc.gpsimd, wf_sc_raw, wf_scales)
 
-        def pf_window(t):
-            return pf_early[t][:] if t < 2 else pf_rest[:, (t - 2) * V : (t - 1) * V]
+        wide_windows = [pf_early[:, V:], pf_early[:, 0:WIDE], pf_rest[:, 0:WIDE]]
 
         picked_all = tile("picked", [P, 7 * HALF], F32)
         picked = {(t, h): picked_all[:, (2 * t + h) * HALF : (2 * t + h + 1) * HALF] for t in range(3) for h in range(2)}
@@ -109,8 +108,11 @@ def tile_list_remainder_on_prototype_pl_kernel(
         def cols(t):
             return slice(t * HALF, (t + 1) * HALF)
 
-        def pick_proto(t, h):
-            nc.vector.tensor_copy(picked[(t, h)], pf_window(t).indirect(half_list(proto_list, h)))
+        def pick_proto(t):
+            nc.vector.tensor_copy(picked_all[:, t * J : (t + 1) * J], wide_windows[t].indirect(proto_list[:]))
+
+        def pick_last_proto(h):
+            nc.vector.tensor_copy(picked[(3, h)], pf_rest[:, V:].indirect(half_list(proto_list, h)))
 
         def remainder(t, h):
             nc.vector.tensor_tensor(
@@ -164,8 +166,7 @@ def tile_list_remainder_on_prototype_pl_kernel(
             nc.sync.dma_start(out=out_words[:, cols(h)], in_=y_codes[h][:].bitcast(I32))
 
         for t in range(2):
-            for h in range(2):
-                pick_proto(t, h)
+            pick_proto(t)
         for h in range(2):
             remainder(0, h)
 
@@ -189,14 +190,14 @@ def tile_list_remainder_on_prototype_pl_kernel(
             for b in range(V // P):
                 nc.tensor.transpose(z_accs[t][:, P * b : P * (b + 1)], zt_sb[b][:, P * t : P * (t + 1)], ident[:])
 
-        for t, h in ((2, 0), (3, 0), (2, 1)):
-            pick_proto(t, h)
+        pick_proto(2)
+        pick_last_proto(0)
         for t, h in ((1, 0), (1, 1), (2, 0), (3, 0)):
             remainder(t, h)
         weave(nc.scalar.copy, diff_bf[0], diff[0][:])
         for t in range(PACK):
             nc.scalar.copy(out=z_sb[t][:], in_=z_accs[t][:])
-        pick_proto(3, 1)
+        pick_last_proto(1)
         deal(wf_dealt[:].bitcast(U16), wf_raw[:].bitcast(U16), 1)
         deal(wf_sc[:], wf_sc_raw, 1)
         nc.vector.quantize_mx(out=d_codes[0][:].bitcast(FP8X4), scales=d_sc[0][:], in_=diff_bf[0])

@@ -92,15 +92,15 @@ def tile_list_remainder_on_prototype_pl_kernel(
         picked[(3, 0)] = picked[(3, 1)] = picked_all[:, 6 * HALF :]
 
         diff = [
-            reuse.tile([P, PACK * HALF], F32, name="diff0", offset=0),
+            reuse.tile([P, PACK * HALF], F32, name="diff0", offset=2 * V),
             tile("diff1", [P, PACK * HALF], F32),
         ]
         th = [tile(f"th{h}", [P, PACK * HALF], F32) for h in range(2)]
         diff_bf = [diff[1][:, 2 * HALF :].bitcast(BF16)]
         d_codes = [tile(f"d_codes{h}", [P, HALF], U32) for h in range(2)]
         d_sc = [tile(f"d_sc{h}", [P, HALF], U8) for h in range(2)]
-        z_sb = [tile(f"z{t}", [P, V], F32) for t in range(2)]
-        z_sb += [reuse.tile([P, V], F32, name=f"z{2 + i}", offset=4 * V * i) for i in range(2)]
+        z_sb = [tile("z0", [P, V], F32)]
+        z_sb += [reuse.tile([P, V], F32, name=f"z{1 + i}", offset=4 * V * i) for i in range(PACK - 1)]
         y = [tile(f"y{h}", [P, PACK * HALF], F32) for h in range(2)]
         y_codes = [tile(f"y_codes{h}", [P, HALF], U32) for h in range(2)]
         y_sc = tile("y_sc", [P, J], U8)
@@ -125,10 +125,10 @@ def tile_list_remainder_on_prototype_pl_kernel(
                 in_=src.rearrange("p (t c i) -> p c t i", i=4, t=PACK),
             )
 
-        def deal(dst, src, width):
+        def deal(dst, src):
             nc.vector.tensor_copy(
-                out=dst.rearrange("p (t m b) -> p m t b", t=PACK, b=width),
-                in_=src.rearrange("p (m t b) -> p m t b", t=PACK, b=width),
+                out=dst.rearrange("p (t m) -> p t m", t=PACK),
+                in_=src.rearrange("p (m t) -> p t m", t=PACK),
             )
 
         def product(t, h):
@@ -161,8 +161,8 @@ def tile_list_remainder_on_prototype_pl_kernel(
                 in_=y[h][:, t0 * HALF : t1 * HALF].rearrange("p (t j) -> p t j", j=HALF),
             )
 
-        def quantise_y(h):
-            nc.vector.quantize_mx(out=y_codes[h][:].bitcast(FP8X4), scales=y_sc[:, cols(h)], in_=y_bf[h][:])
+        def quantise_y(h, src):
+            nc.vector.quantize_mx(out=y_codes[h][:].bitcast(FP8X4), scales=y_sc[:, cols(h)], in_=src)
             nc.sync.dma_start(out=out_words[:, cols(h)], in_=y_codes[h][:].bitcast(I32))
 
         for t in range(2):
@@ -170,7 +170,7 @@ def tile_list_remainder_on_prototype_pl_kernel(
         for h in range(2):
             remainder(0, h)
 
-        zt_sb = [tile(f"zt{b}", [P, N], F32) for b in range(V // P)]
+        zt_sb = [tile(f"zt{b}", [P, N], F32)[:] for b in range(V // P - 1)] + [diff[1][:, 2 * HALF :]]
         for b in range(V // P):
             acc = ps.tile([P, N], F32, name=f"zt_acc{b}", tag=f"bank{b}")
             nc.tensor.matmul_mx(
@@ -183,7 +183,7 @@ def tile_list_remainder_on_prototype_pl_kernel(
                 stop=True,
             )
             nc.scalar.copy(
-                out=zt_sb[b][:].rearrange("p (t m) -> p t m", t=PACK), in_=acc[:].rearrange("p (m t) -> p t m", t=PACK)
+                out=zt_sb[b].rearrange("p (t m) -> p t m", t=PACK), in_=acc[:].rearrange("p (m t) -> p t m", t=PACK)
             )
         z_accs = [ps.tile([P, V], F32, name=f"z_acc{t}", tag=f"bank{t}") for t in range(PACK)]
         for t in range(PACK):
@@ -194,12 +194,13 @@ def tile_list_remainder_on_prototype_pl_kernel(
         pick_last_proto(0)
         for t, h in ((1, 0), (1, 1), (2, 0), (3, 0)):
             remainder(t, h)
+        nc.scalar.copy(out=z_sb[0][:], in_=z_accs[0][:])
         weave(nc.scalar.copy, diff_bf[0], diff[0][:])
-        for t in range(PACK):
+        for t in range(1, PACK):
             nc.scalar.copy(out=z_sb[t][:], in_=z_accs[t][:])
         pick_last_proto(1)
-        deal(wf_dealt[:].bitcast(U16), wf_raw[:].bitcast(U16), 1)
-        deal(wf_sc[:], wf_sc_raw, 1)
+        deal(wf_dealt[:].bitcast(U16), wf_raw[:].bitcast(U16))
+        deal(wf_sc[:], wf_sc_raw)
         nc.vector.quantize_mx(out=d_codes[0][:].bitcast(FP8X4), scales=d_sc[0][:], in_=diff_bf[0])
         remainder(2, 1)
         remainder(3, 1)
@@ -221,15 +222,16 @@ def tile_list_remainder_on_prototype_pl_kernel(
         accs = [product(t, 1) for t in range(PACK)]
         for t in range(PACK):
             squash(t, 1, accs[t])
-        y_bf = [tile("y_bf0", [P, PACK * HALF], BF16, tag="d_codes1"), tile("y_bf1", [P, PACK * HALF], BF16)]
-        weave(nc.scalar.copy, y_bf[0][:], y[0][:])
+        y_bf = tile("y_bf0", [P, PACK * HALF], BF16, tag="d_codes1")
+        weave(nc.scalar.copy, y_bf[:], y[0][:])
         for t in range(PACK):
             add_features(t, 1)
             if t % 2 == 1:
                 store_y(1, t - 1, t + 1)
-        quantise_y(0)
-        weave(nc.vector.tensor_copy, y_bf[1][:], y[1][:])
-        quantise_y(1)
+        quantise_y(0, y_bf[:])
+        y_bf1 = tile("y_bf1", [P, PACK * HALF], BF16)
+        weave(nc.vector.tensor_copy, y_bf1[:], y[1][:])
+        quantise_y(1, y_bf1[:])
         for q in range(4):
             queue = nc.sync if q % 2 else nc.scalar
             queue.dma_start(

@@ -49,7 +49,6 @@ def tile_list_remainder_on_prototype_pl_kernel(
         pq_sc = tile("pq_sc", [P, V], U8)[:]
         ident = tile("ident", [P, P], F32)
         wf_dealt = tile("wf_dealt", [P, 2 * N], U8)
-        wf_sc = tile("wf_sc", [P, N], U8)
         warm = tile("warm", [P, 2], F32)
 
         def half_list(lst, h):
@@ -87,9 +86,12 @@ def tile_list_remainder_on_prototype_pl_kernel(
 
         wide_windows = [pf_early[:, V:], pf_early[:, 0:WIDE], pf_rest[:, 0:WIDE]]
 
-        picked_all = tile("picked", [P, 7 * HALF], F32)
+        picked_all = tile("picked", [P, 6 * HALF], F32)
         picked = {(t, h): picked_all[:, (2 * t + h) * HALF : (2 * t + h + 1) * HALF] for t in range(3) for h in range(2)}
-        picked[(3, 0)] = picked[(3, 1)] = picked_all[:, 6 * HALF :]
+        late = (PACK - 1) * 4 * V
+        picked[(3, 0)] = reuse.tile([P, HALF], F32, name="picked30", offset=late + N // 2)[:]
+        wf_sc = reuse.tile([P, N], U8, name="wf_sc", offset=late, align_bytes=64)
+        picked[(3, 1)] = reuse.tile([P, HALF], F32, name="picked31", offset=late + N)[:]
 
         diff = [
             reuse.tile([P, PACK * HALF], F32, name="diff0", offset=2 * V),
@@ -121,8 +123,8 @@ def tile_list_remainder_on_prototype_pl_kernel(
 
         def weave(copy, dst, src):
             copy(
-                out=dst.rearrange("p (c i t) -> p c t i", i=4, t=PACK),
-                in_=src.rearrange("p (t c i) -> p c t i", i=4, t=PACK),
+                out=dst.rearrange("p (c i t) -> p c t i", i=2, t=PACK),
+                in_=src.rearrange("p (t c i) -> p c t i", i=2, t=PACK),
             )
 
         def deal(dst, src):

from contextlib import ExitStack

import concourse.mybir as mybir
from concourse.masks import make_identity

K, V, T, J, N = 512, 512, 1024, 512, 512
FLOPS = 2 * K * N * (V + J)

F32 = mybir.dt.float32
BF16 = mybir.dt.bfloat16
I32 = mybir.dt.int32
U32 = mybir.dt.uint32
U16 = mybir.dt.uint16
U8 = mybir.dt.uint8
FP8X4 = mybir.dt.float8_e4m3fn_x4
FP4X4 = mybir.dt.float4_e2m1fn_x4
ALU = mybir.AluOpType
TANH = mybir.ActivationFunctionType.Tanh

P = 128
PACK = 4
HALF = J // 2
STRIPE = 16
WIDE = 704


def tile_list_remainder_on_prototype_pl_kernel(
    tc, pq_words, pq_scales, wq_words, wq_scales, xf, pf, wf_words, wf_scales, offs, offs2, out_0, out_1, out_2
):
    nc = tc.nc
    with ExitStack() as ctx:
        sb = ctx.enter_context(tc.tile_pool(name="sb", bufs=1))
        reuse = ctx.enter_context(tc.tile_pool(name="reuse", bufs=1))
        ps = ctx.enter_context(tc.psum_pool(name="ps", bufs=2))

        def tile(name, shape, dtype, tag=None):
            return sb.tile(shape, dtype, name=name, tag=tag or name, align_bytes=64)

        tok_list = tile("tok_list", [P, J // STRIPE], U16)
        proto_list = tile("proto_list", [P, J // STRIPE], U16)
        pf_early = tile("pf_early", [P, V + WIDE], F32)
        pf_rest = tile("pf_rest", [P, 2 * V], F32)
        xf_sb = [tile(f"xf{t}", [P, T], F32) for t in range(PACK)]
        wq_sb = tile("wq_sb", [P, N], U32)
        wf_raw = tile("wf_raw", [P, 2 * N], U8)
        pq_sb = tile("pq_sb", [P, 2 * V], U8)
        wf_sc_raw = tile("wf_sc_raw", [P, N], U8)[:]
        wq_sc = tile("wq_sc", [P, N], U8)[:]
        pq_sc = tile("pq_sc", [P, V], U8)[:]
        ident = tile("ident", [P, P], F32)
        wf_dealt = tile("wf_dealt", [P, 2 * N], U8)
        warm = tile("warm", [P, 2], F32)

        def half_list(lst, h):
            cols = HALF // STRIPE
            return lst[:, h * cols : (h + 1) * cols]

        def load_scales(dst, src, quadrants=range(4)):
            for q in quadrants:
                nc.sync.dma_start(out=dst[32 * q : 32 * q + 4, :].bitcast(I32), in_=src[0, 4 * q : 4 * q + 4, :].bitcast(I32))

        nc.vector.memset(wf_sc_raw.bitcast(I32), 0)
        nc.vector.memset(warm[:, 0:1], 0.0)
        nc.vector.memset(pf_early[:, 2 * V :], 0.0)

        pf_rows = pf.rearrange("(p t) v -> p (t v)", t=PACK)
        xf_rows = xf.rearrange("(p t) c -> p t c", t=PACK)
        nc.sync.dma_start(out=pf_early[:, V : 2 * V], in_=pf_rows[:, 0:V])
        nc.sync.dma_start(proto_list[:], offs2)
        load_scales(wq_sc, wq_scales, range(3))
        nc.sync.dma_start(out=pf_early[:, 0:V], in_=pf_rows[:, V : 2 * V])
        nc.sync.dma_start(tok_list[:], offs)
        nc.sync.dma_start(out=xf_sb[0][:], in_=xf_rows[:, 0, :])
        load_scales(wq_sc, wq_scales, range(3, 4))
        nc.sync.dma_start(out=pf_rest[:], in_=pf_rows[:, 2 * V :])
        load_scales(pq_sc, pq_scales)
        nc.sync.dma_start(out=wq_sb[:].bitcast(I32), in_=wq_words[0].rearrange("p n r -> p (n r)").bitcast(I32))
        nc.sync.dma_start(out=pq_sb[:].bitcast(I32), in_=pq_words[0].bitcast(I32))
        for t in range(1, 3):
            nc.sync.dma_start(out=xf_sb[t][:], in_=xf_rows[:, t, :])
        load_scales(wf_sc_raw, wf_scales)
        nc.sync.dma_start(out=xf_sb[3][:], in_=xf_rows[:, 3, :])
        nc.sync.dma_start(out=wf_raw[:].bitcast(I32), in_=wf_words[0].bitcast(I32))
        nc.scalar.activation(out=warm[:, 1:2], in_=warm[:, 0:1], func=TANH)
        make_identity(nc, ident[:])

        wide_windows = [pf_early[:, V:], pf_early[:, 0:WIDE], pf_rest[:, 0:WIDE]]

        picked_all = tile("picked", [P, 6 * HALF], F32)
        picked = {(t, h): picked_all[:, (2 * t + h) * HALF : (2 * t + h + 1) * HALF] for t in range(3) for h in range(2)}
        late = (PACK - 1) * 4 * V
        picked[(3, 0)] = reuse.tile([P, HALF], F32, name="picked30", offset=late + N // 2)[:]
        wf_sc = reuse.tile([P, N], U8, name="wf_sc", offset=late, align_bytes=64)
        picked[(3, 1)] = reuse.tile([P, HALF], F32, name="picked31", offset=late + N)[:]

        diff = [
            reuse.tile([P, PACK * HALF], F32, name="diff0", offset=2 * V),
            tile("diff1", [P, PACK * HALF], F32),
        ]
        th = [tile(f"th{h}", [P, PACK * HALF], F32) for h in range(2)]
        diff_bf = [diff[1][:, 2 * HALF :].bitcast(BF16)]
        d_codes = [tile(f"d_codes{h}", [P, HALF], U32) for h in range(2)]
        d_sc = [tile(f"d_sc{h}", [P, HALF], U8) for h in range(2)]
        z_sb = [tile("z0", [P, V], F32)]
        z_sb += [reuse.tile([P, V], F32, name=f"z{1 + i}", offset=4 * V * i) for i in range(PACK - 1)]
        y = [tile(f"y{h}", [P, PACK * HALF], F32) for h in range(2)]
        y_codes = [tile(f"y_codes{h}", [P, HALF], U32) for h in range(2)]
        y_sc = tile("y_sc", [P, J], U8)

        def cols(t):
            return slice(t * HALF, (t + 1) * HALF)

        def pick_proto(t):
            nc.vector.tensor_copy(picked_all[:, t * J : (t + 1) * J], wide_windows[t].indirect(proto_list[:]))

        def pick_last_proto(h):
            nc.vector.tensor_copy(picked[(3, h)], pf_rest[:, V:].indirect(half_list(proto_list, h)))

        def remainder(t, h):
            nc.vector.tensor_tensor(
                diff[h][:, cols(t)], xf_sb[t][:].indirect(half_list(tok_list, h)), picked[(t, h)], ALU.subtract
            )

        def weave(copy, dst, src):
            copy(
                out=dst.rearrange("p (c i t) -> p c t i", i=2, t=PACK),
                in_=src.rearrange("p (t c i) -> p c t i", i=2, t=PACK),
            )

        def deal(dst, src):
            nc.vector.tensor_copy(
                out=dst.rearrange("p (t m) -> p t m", t=PACK),
                in_=src.rearrange("p (m t) -> p t m", t=PACK),
            )

        def product(t, h):
            acc = ps.tile([P, HALF], F32, name=f"p{t}{h}", tag=f"bank{t}")
            nc.tensor.matmul_mx(
                out=acc[:],
                lhsT=wf_dealt[:, 2 * P * t : 2 * P * (t + 1)].bitcast(FP4X4),
                lhsT_scale=wf_sc[:, P * t : P * (t + 1)],
                rhs=d_codes[h][:].bitcast(FP8X4),
                rhs_scale=d_sc[h][:],
                start=True,
                stop=True,
            )
            return acc

        def squash(t, h, acc):
            nc.scalar.activation(out=th[h][:, cols(t)], in_=acc[:], func=TANH)

        def add_features(t, h):
            nc.vector.tensor_tensor(
                y[h][:, cols(t)], z_sb[t][:].indirect(half_list(proto_list, h)), th[h][:, cols(t)], ALU.add
            )

        out_rows = out_0.rearrange("(p t) j -> p t j", t=PACK)
        out_words = out_1[0].rearrange("p c r -> p (c r)").bitcast(I32)

        def store_y(h, t0, t1):
            nc.sync.dma_start(
                out=out_rows[:, t0:t1, cols(h)],
                in_=y[h][:, t0 * HALF : t1 * HALF].rearrange("p (t j) -> p t j", j=HALF),
            )

        def quantise_y(h, src):
            nc.vector.quantize_mx(out=y_codes[h][:].bitcast(FP8X4), scales=y_sc[:, cols(h)], in_=src)
            nc.sync.dma_start(out=out_words[:, cols(h)], in_=y_codes[h][:].bitcast(I32))

        for t in range(2):
            pick_proto(t)
        for h in range(2):
            remainder(0, h)

        zt_sb = [tile(f"zt{b}", [P, N], F32)[:] for b in range(V // P - 1)] + [diff[1][:, 2 * HALF :]]
        for b in range(V // P):
            acc = ps.tile([P, N], F32, name=f"zt_acc{b}", tag=f"bank{b}")
            nc.tensor.matmul_mx(
                out=acc[:],
                lhsT=pq_sb[:, 2 * P * b : 2 * P * (b + 1)].bitcast(FP4X4),
                lhsT_scale=pq_sc[:, P * b : P * (b + 1)],
                rhs=wq_sb[:].bitcast(FP8X4),
                rhs_scale=wq_sc,
                start=True,
                stop=True,
            )
            nc.scalar.copy(
                out=zt_sb[b].rearrange("p (t m) -> p t m", t=PACK), in_=acc[:].rearrange("p (m t) -> p t m", t=PACK)
            )
        z_accs = [ps.tile([P, V], F32, name=f"z_acc{t}", tag=f"bank{t}") for t in range(PACK)]
        for t in range(PACK):
            for b in range(V // P):
                nc.tensor.transpose(z_accs[t][:, P * b : P * (b + 1)], zt_sb[b][:, P * t : P * (t + 1)], ident[:])

        pick_proto(2)
        pick_last_proto(0)
        for t, h in ((1, 0), (1, 1), (2, 0), (3, 0)):
            remainder(t, h)
        nc.scalar.copy(out=z_sb[0][:], in_=z_accs[0][:])
        weave(nc.scalar.copy, diff_bf[0], diff[0][:])
        for t in range(1, PACK):
            nc.scalar.copy(out=z_sb[t][:], in_=z_accs[t][:])
        pick_last_proto(1)
        deal(wf_dealt[:].bitcast(U16), wf_raw[:].bitcast(U16))
        deal(wf_sc[:], wf_sc_raw)
        nc.vector.quantize_mx(out=d_codes[0][:].bitcast(FP8X4), scales=d_sc[0][:], in_=diff_bf[0])
        remainder(2, 1)
        remainder(3, 1)

        accs = [product(t, 0) for t in range(PACK)]
        squash(0, 0, accs[0])
        add_features(0, 0)
        squash(1, 0, accs[1])
        diff_bf.append(tile("diff_bf1", [P, PACK * HALF], BF16, tag="d_codes0")[:])
        weave(nc.scalar.copy, diff_bf[1], diff[1][:])
        squash(2, 0, accs[2])
        squash(3, 0, accs[3])
        add_features(1, 0)
        nc.vector.quantize_mx(out=d_codes[1][:].bitcast(FP8X4), scales=d_sc[1][:], in_=diff_bf[1])
        add_features(2, 0)
        add_features(3, 0)
        store_y(0, 0, PACK)

        accs = [product(t, 1) for t in range(PACK)]
        for t in range(PACK):
            squash(t, 1, accs[t])
        y_bf = tile("y_bf0", [P, PACK * HALF], BF16, tag="d_codes1")
        weave(nc.scalar.copy, y_bf[:], y[0][:])
        for t in range(PACK):
            add_features(t, 1)
            if t % 2 == 1:
                store_y(1, t - 1, t + 1)
        quantise_y(0, y_bf[:])
        y_bf1 = tile("y_bf1", [P, PACK * HALF], BF16)
        weave(nc.vector.tensor_copy, y_bf1[:], y[1][:])
        quantise_y(1, y_bf1[:])
        for q in range(4):
            queue = nc.sync if q % 2 else nc.scalar
            queue.dma_start(
                out=out_2[0, 4 * q : 4 * q + 4, :].bitcast(I32), in_=y_sc[32 * q : 32 * q + 4, :].bitcast(I32)
            )
